import numpy as np
import ml_dtypes


def mxq(x, axis, fmt="e4m3"):
    dtype, down = {"e4m3": (ml_dtypes.float8_e4m3fn, 7), "e5m2": (ml_dtypes.float8_e5m2, 14)}[fmt]
    v = np.moveaxis(np.asarray(x, np.float32).astype(ml_dtypes.bfloat16).astype(np.float64), axis, -1)
    blocks = v.reshape(v.shape[:-1] + (-1, 32))
    amax = np.abs(blocks).max(-1, keepdims=True)
    byte = np.maximum(np.where(amax > 0, np.frexp(amax)[1] - 1 + 127, 0) - down, 1)
    scale = np.exp2(byte - 127.0)
    codes = (blocks / scale).astype(np.float32).astype(dtype).astype(np.float64)
    return np.moveaxis((codes * scale).reshape(v.shape), -1, axis)


WIDE = False


def mx_kscale(k):
    if not WIDE:
        return np.ones(k)
    levels = np.array([10, -10, 5, -5, 0])
    if k % 512:
        return np.exp2(np.random.permutation(np.resize(levels, k // 32))).repeat(32)
    a = np.empty((k // 512, 16))
    for p in range(k // 512):
        a[p, :8] = np.random.permutation(np.resize(levels, 8))
        for g in range(8):
            far = levels[np.abs(levels - a[p, g]) >= 10]
            a[p, g + 8] = far[np.random.randint(len(far))]
    return np.exp2(a.ravel()).repeat(32)


def f64(x):
    return np.asarray(x).astype(np.float64)


def striped(idx):
    return np.tile(idx.reshape(-1, 16).T, (8, 1)).astype(np.uint16)


def unstriped(offs):
    return offs[:16].T.reshape(-1).astype(np.int64)


E2M1 = np.array([0.0, 0.5, 1.0, 1.5, 2.0, 3.0, 4.0, 6.0, -0.0, -0.5, -1.0, -1.5, -2.0, -3.0, -4.0, -6.0])


def pack_weight(w, fmt):
    k, n = w.shape
    w = f64(np.asarray(w, np.float32).astype(ml_dtypes.bfloat16)).reshape(k // 32, 32, n)
    amax = np.abs(w).max(1)
    if fmt == "e4m3":
        byte = np.frexp(amax)[1] - 1 + 127 - 7
    else:
        mant, ex = np.frexp(amax / 6.0)
        byte = np.where(mant > 0.5, ex, ex - 1) + 127
    byte = np.clip(np.where(amax > 0, byte, 1), 1, 254)
    scaled = (w * np.exp2(127.0 - byte)[:, None, :]).reshape(k, n).astype(np.float32)
    by_word = np.ascontiguousarray(scaled.reshape(k // 512, 128, 4, n).transpose(0, 1, 3, 2))
    if fmt == "e4m3":
        words = by_word.astype(ml_dtypes.float8_e4m3fn).view(np.uint8)
    else:
        c = by_word.astype(ml_dtypes.float4_e2m1fn).view(np.uint8) & 0xF
        words = (c[..., 0::2] | (c[..., 1::2] << 4)).reshape(k // 512, 128, 2 * n)
    return np.ascontiguousarray(words), np.ascontiguousarray(byte.astype(np.uint8).reshape(k // 512, 16, n))


def unpack_weight(words, scales, fmt):
    g, _, n = scales.shape
    words = np.ascontiguousarray(words).reshape(g, 128, n, -1)
    if fmt == "e4m3":
        vals = words.view(ml_dtypes.float8_e4m3fn).astype(np.float64)
    else:
        nib = np.empty((g, 128, n, 4), np.uint8)
        nib[..., 0::2] = words & 0xF
        nib[..., 1::2] = words >> 4
        vals = E2M1[nib]
    vals = vals * np.repeat(np.exp2(scales.astype(np.float64) - 127.0), 8, axis=1)[..., None]
    return vals.transpose(0, 1, 3, 2).reshape(g * 512, n)


def pack_table(v):
    words, scales = pack_weight(v, "e4m3")
    return np.concatenate([words.reshape(words.shape[0], -1), scales.reshape(scales.shape[0], -1)], axis=1)


def unpack_table(tab):
    g, t = tab.shape[0], tab.shape[1] // 528
    return unpack_weight(tab[:, :512 * t].reshape(g, 128, t, 4), tab[:, 512 * t:].reshape(g, 16, t), "e4m3")


O, K, M, T, S = 512, 1024, 256, 1024, 512


def setup_inputs():
    n = np.random.standard_normal
    s = mx_kscale(K)[:, None]
    w = n((K, M)) / np.sqrt(K) / s
    p_w4 = pack_weight(w[O:], "e2m1")
    return {
        "tab": pack_table(n((K, T)) * s),
        "w8": (w[:O]).astype(np.float32),
        "w4_words": p_w4[0],
        "w4_scales": p_w4[1],
        "offs": striped(np.random.permutation(T)[:S]),
    }


def reference(tab, w8, w4_words, w4_scales, offs):
    tab_ = unpack_table(tab)[:, unstriped(offs)]
    w8_ = mxq(f64(w8), 0, "e4m3")
    w4_ = unpack_weight(w4_words, w4_scales, "e2m1")
    y = w8_.T @ tab_[:O] + w4_.T @ tab_[O:]
    return y

@@ -1,0 +1,103 @@
+from contextlib import ExitStack
+
+import concourse.mybir as mybir
+
+F32 = mybir.dt.float32
+BF16 = mybir.dt.bfloat16
+U32 = mybir.dt.uint32
+I32 = mybir.dt.int32
+U16 = mybir.dt.uint16
+U8 = mybir.dt.uint8
+E4M3 = mybir.dt.float8_e4m3fn_x4
+E2M1 = mybir.dt.float4_e2m1fn_x4
+COPY = mybir.ActivationFunctionType.Copy
+
+O, K, M, T, S = 512, 1024, 256, 1024, 512
+P = 128
+PACK = 4
+FLOPS = 2 * K * M * S
+
+
+def tile_list_tabo_none_kernel(tc, tab, w8, w4_words, w4_scales, offs, out):
+    nc = tc.nc
+    with ExitStack() as ctx:
+        keep = ctx.enter_context(tc.tile_pool(name="keep", bufs=1))
+        psum = ctx.enter_context(tc.psum_pool(name="psum", bufs=1))
+
+        offsets = keep.tile([P, S // 16], U16, name="offsets")
+        words = [keep.tile([P, T], I32, name=f"words{a}", align_bytes=64) for a in range(2)]
+        planes = keep.tile([P, T], U8, name="planes", align_bytes=64)
+        w8_raw = keep.tile([P, PACK, M], F32, name="w8_raw", align_bytes=64)
+        w8_grouped = keep.tile([P, M, PACK], BF16, name="w8_grouped", align_bytes=64)
+        w8_codes = keep.tile([P, M], U32, name="w8_codes", align_bytes=64)
+        w8_plane = keep.tile([P, M], U8, name="w8_plane", align_bytes=64)
+        w4_codes = keep.tile([P, 2 * M], U8, name="w4_codes", align_bytes=64)
+        w4_plane = keep.tile([P, M], U8, name="w4_plane", align_bytes=64)
+        picked = [keep.tile([P, S], U32, name=f"picked{a}", align_bytes=64) for a in range(2)]
+        picked_planes = keep.tile([P, S], U8, name="picked_planes", align_bytes=64)
+        warm = keep.tile([P, 1], F32, name="warm")
+        results = [keep.tile([P, S], F32, name=f"result{m}", align_bytes=64) for m in range(2)]
+        sums = [psum.tile([P, S], F32, name=f"sum{m}") for m in range(2)]
+
+        table_words = [tab[a, 0 : 4 * P * T].rearrange("(p b) -> p b", b=4 * T).bitcast(I32) for a in range(2)]
+        table_scales = [tab[a, 4 * P * T : 4 * P * T + 16 * T].rearrange("(q t) -> q t", t=T).bitcast(I32) for a in range(2)]
+
+        nc.vector.memset(planes[:].bitcast(I32), 0)
+        nc.gpsimd.memset(w4_plane[:].bitcast(I32), 0)
+
+        nc.sync.dma_start(offsets[:], offs)
+        nc.sync.dma_start(words[1][:], table_words[1])
+        nc.sync.dma_start(w8_raw[:], w8.rearrange("(p j) n -> p j n", j=PACK))
+        nc.sync.dma_start(words[0][:], table_words[0])
+
+        for q in range(4):
+            nc.scalar.dma_start(planes[32 * q : 32 * q + 4, :].bitcast(I32), table_scales[1][4 * q : 4 * q + 4, :])
+        for q in range(4):
+            nc.gpsimd.dma_start(planes[32 * q + 4 : 32 * q + 8, :].bitcast(I32), table_scales[0][4 * q : 4 * q + 4, :])
+        nc.gpsimd.dma_start(w4_codes[:].bitcast(I32), w4_words[0].bitcast(I32))
+        for q in range(4):
+            nc.gpsimd.dma_start(w4_plane[32 * q : 32 * q + 4, :].bitcast(I32), w4_scales[0, 4 * q : 4 * q + 4, :].bitcast(I32))
+
+        nc.vector.memset(warm[:], 0.0)
+        nc.scalar.activation(warm[:], warm[:], COPY)
+
+        nc.vector.tensor_copy(picked[1][:], words[1][:].bitcast(U32).indirect(offsets[:]))
+        nc.vector.tensor_copy(picked_planes[:], planes[:].indirect(offsets[:]))
+        for m in range(2):
+            cols = slice(m * P, (m + 1) * P)
+            nc.scalar.copy(w8_grouped[:, cols, :], w8_raw[:, :, cols].rearrange("p j n -> p n j"))
+        for m in range(2):
+            cols = slice(m * P, (m + 1) * P)
+            nc.vector.quantize_mx(
+                out=w8_codes[:, cols].bitcast(E4M3),
+                scales=w8_plane[:, cols],
+                in_=w8_grouped[:, cols, :].rearrange("p n j -> p (n j)"),
+            )
+        nc.vector.tensor_copy(picked[0][:], words[0][:].bitcast(U32).indirect(offsets[:]))
+
+        for m in range(2):
+            cols = slice(m * P, (m + 1) * P)
+            nc.tensor.matmul_mx(
+                out=sums[m][:],
+                lhsT=w4_codes[:, 2 * m * P : 2 * (m + 1) * P].bitcast(E2M1),
+                lhsT_scale=w4_plane[:, cols],
+                rhs=picked[1][:].bitcast(E4M3),
+                rhs_scale=picked_planes[:],
+                start=True,
+                stop=False,
+            )
+        for m in range(2):
+            cols = slice(m * P, (m + 1) * P)
+            nc.tensor.matmul_mx(
+                out=sums[m][:],
+                lhsT=w8_codes[:, cols].bitcast(E4M3),
+                lhsT_scale=w8_plane[:, cols],
+                rhs=picked[0][:].bitcast(E4M3),
+                rhs_scale=picked_planes[4:P, :],
+                start=False,
+                stop=True,
+            )
+        nc.scalar.copy(results[0][:], sums[0][:])
+        nc.vector.tensor_copy(results[1][:], sums[1][:])
+        nc.scalar.dma_start(out[0:P, :], results[0][:])
+        nc.sync.dma_start(out[P : 2 * P, :], results[1][:])

@@ -37,28 +37,26 @@ def tile_list_tabo_none_kernel(tc, tab, w8, w4_words, w4_scales, offs, out):
         picked_planes = keep.tile([P, S], U8, name="picked_planes", align_bytes=64)
         warm = keep.tile([P, 1], F32, name="warm")
         results = [keep.tile([P, S], F32, name=f"result{m}", align_bytes=64) for m in range(2)]
-        sums = [psum.tile([P, S], F32, name=f"sum{m}") for m in range(2)]
+        sums = [[psum.tile([P, P], F32, name=f"sum{m}_{c}") for c in range(4)] for m in range(2)]
 
         table_words = [tab[a, 0 : 4 * P * T].rearrange("(p b) -> p b", b=4 * T).bitcast(I32) for a in range(2)]
         table_scales = [tab[a, 4 * P * T : 4 * P * T + 16 * T].rearrange("(q t) -> q t", t=T).bitcast(I32) for a in range(2)]
 
         nc.vector.memset(planes[:].bitcast(I32), 0)
-        nc.gpsimd.memset(w4_plane[:].bitcast(I32), 0)
+        nc.vector.memset(warm[:], 0.0)
 
+        for q in range(4):
+            nc.scalar.dma_start(planes[32 * q : 32 * q + 4, :].bitcast(I32), table_scales[1][4 * q : 4 * q + 4, :])
         nc.sync.dma_start(offsets[:], offs)
         nc.sync.dma_start(words[1][:], table_words[1])
         nc.sync.dma_start(w8_raw[:], w8.rearrange("(p j) n -> p j n", j=PACK))
         nc.sync.dma_start(words[0][:], table_words[0])
-
         for q in range(4):
-            nc.scalar.dma_start(planes[32 * q : 32 * q + 4, :].bitcast(I32), table_scales[1][4 * q : 4 * q + 4, :])
-        for q in range(4):
-            nc.gpsimd.dma_start(planes[32 * q + 4 : 32 * q + 8, :].bitcast(I32), table_scales[0][4 * q : 4 * q + 4, :])
-        nc.gpsimd.dma_start(w4_codes[:].bitcast(I32), w4_words[0].bitcast(I32))
+            nc.scalar.dma_start(planes[32 * q + 4 : 32 * q + 8, :].bitcast(I32), table_scales[0][4 * q : 4 * q + 4, :])
         for q in range(4):
             nc.gpsimd.dma_start(w4_plane[32 * q : 32 * q + 4, :].bitcast(I32), w4_scales[0, 4 * q : 4 * q + 4, :].bitcast(I32))
 
-        nc.vector.memset(warm[:], 0.0)
+        nc.scalar.dma_start(w4_codes[:].bitcast(I32), w4_words[0].bitcast(I32))
         nc.scalar.activation(warm[:], warm[:], COPY)
 
         nc.vector.tensor_copy(picked[1][:], words[1][:].bitcast(U32).indirect(offsets[:]))
@@ -73,31 +71,38 @@ def tile_list_tabo_none_kernel(tc, tab, w8, w4_words, w4_scales, offs, out):
                 scales=w8_plane[:, cols],
                 in_=w8_grouped[:, cols, :].rearrange("p n j -> p (n j)"),
             )
-        nc.vector.tensor_copy(picked[0][:], words[0][:].bitcast(U32).indirect(offsets[:]))
 
-        for m in range(2):
-            cols = slice(m * P, (m + 1) * P)
-            nc.tensor.matmul_mx(
-                out=sums[m][:],
-                lhsT=w4_codes[:, 2 * m * P : 2 * (m + 1) * P].bitcast(E2M1),
-                lhsT_scale=w4_plane[:, cols],
-                rhs=picked[1][:].bitcast(E4M3),
-                rhs_scale=picked_planes[:],
-                start=True,
-                stop=False,
-            )
-        for m in range(2):
-            cols = slice(m * P, (m + 1) * P)
-            nc.tensor.matmul_mx(
-                out=sums[m][:],
-                lhsT=w8_codes[:, cols].bitcast(E4M3),
-                lhsT_scale=w8_plane[:, cols],
-                rhs=picked[0][:].bitcast(E4M3),
-                rhs_scale=picked_planes[4:P, :],
-                start=False,
-                stop=True,
-            )
-        nc.scalar.copy(results[0][:], sums[0][:])
-        nc.vector.tensor_copy(results[1][:], sums[1][:])
-        nc.scalar.dma_start(out[0:P, :], results[0][:])
-        nc.sync.dma_start(out[P : 2 * P, :], results[1][:])
+        for c in range(4):
+            for m in range(2):
+                nc.tensor.matmul_mx(
+                    out=sums[m][c][:],
+                    lhsT=w4_codes[:, 2 * m * P : 2 * (m + 1) * P].bitcast(E2M1),
+                    lhsT_scale=w4_plane[:, m * P : (m + 1) * P],
+                    rhs=picked[1][:, c * P : (c + 1) * P].bitcast(E4M3),
+                    rhs_scale=picked_planes[:, c * P : (c + 1) * P],
+                    start=True,
+                    stop=False,
+                )
+        for c in range(4):
+            cols = slice(c * P, (c + 1) * P)
+            nc.vector.tensor_copy(picked[0][:, cols], words[0][:].bitcast(U32).indirect(offsets[:, 8 * c : 8 * (c + 1)]))
+            for m in range(2):
+                nc.tensor.matmul_mx(
+                    out=sums[m][c][:],
+                    lhsT=w8_codes[:, m * P : (m + 1) * P].bitcast(E4M3),
+                    lhsT_scale=w8_plane[:, m * P : (m + 1) * P],
+                    rhs=picked[0][:, cols].bitcast(E4M3),
+                    rhs_scale=picked_planes[4:P, cols],
+                    start=False,
+                    stop=True,
+                )
+            nc.scalar.copy(results[0][:, cols], sums[0][c][:])
+            if c < 3:
+                nc.scalar.copy(results[1][:, cols], sums[1][c][:])
+            else:
+                nc.vector.tensor_copy(results[1][:, cols], sums[1][c][:])
+            if c == 2:
+                for m in range(2):
+                    nc.sync.dma_start(out[m * P : (m + 1) * P, 0 : 3 * P], results[m][:, 0 : 3 * P])
+        nc.scalar.dma_start(out[0:P, 3 * P : S], results[0][:, 3 * P : S])
+        nc.sync.dma_start(out[P : 2 * P, 3 * P : S], results[1][:, 3 * P : S])

@@ -42,57 +42,69 @@ def tile_list_tabo_none_kernel(tc, tab, w8, w4_words, w4_scales, offs, out):
         table_words = [tab[a, 0 : 4 * P * T].rearrange("(p b) -> p b", b=4 * T).bitcast(I32) for a in range(2)]
         table_scales = [tab[a, 4 * P * T : 4 * P * T + 16 * T].rearrange("(q t) -> q t", t=T).bitcast(I32) for a in range(2)]
 
-        nc.vector.memset(planes[:].bitcast(I32), 0)
         nc.vector.memset(warm[:], 0.0)
 
-        for q in range(4):
-            nc.scalar.dma_start(planes[32 * q : 32 * q + 4, :].bitcast(I32), table_scales[1][4 * q : 4 * q + 4, :])
-        nc.sync.dma_start(offsets[:], offs)
-        nc.sync.dma_start(words[1][:], table_words[1])
-        nc.sync.dma_start(w8_raw[:], w8.rearrange("(p j) n -> p j n", j=PACK))
-        nc.sync.dma_start(words[0][:], table_words[0])
-        for q in range(4):
-            nc.scalar.dma_start(planes[32 * q + 4 : 32 * q + 8, :].bitcast(I32), table_scales[0][4 * q : 4 * q + 4, :])
-        for q in range(4):
-            nc.gpsimd.dma_start(w4_plane[32 * q : 32 * q + 4, :].bitcast(I32), w4_scales[0, 4 * q : 4 * q + 4, :].bitcast(I32))
+        flat = tab.rearrange("a b -> (a b)")
 
-        nc.scalar.dma_start(w4_codes[:].bitcast(I32), w4_words[0].bitcast(I32))
+        def load_scales(queue, a, q, before, rows):
+            first = 32 * q + 4 * (1 - a) - before
+            start = a * (4 * P + 16) * T + 4 * P * T + (4 * q - before) * T
+            queue.dma_start(
+                planes[first : first + rows, :].bitcast(I32),
+                flat[start : start + rows * T].rearrange("(r t) -> r t", t=T).bitcast(I32),
+            )
+
+        def load_w4_scales(queue, q):
+            queue.dma_start(w4_plane[32 * q : 32 * q + 4, :].bitcast(I32), w4_scales[0, 4 * q : 4 * q + 4, :].bitcast(I32))
+
+        nc.vector.memset(planes[96:P, :].bitcast(I32), 0)
+        nc.sync.dma_start(offsets[:], offs)
+        load_scales(nc.scalar, 1, 0, 0, 4)
+        load_scales(nc.sync, 1, 1, 12, 16)
+        load_scales(nc.scalar, 1, 2, 12, 16)
+        load_scales(nc.sync, 0, 0, 0, 16)
+        load_scales(nc.scalar, 1, 3, 12, 16)
+        nc.sync.dma_start(words[0][:], table_words[0])
+        load_scales(nc.scalar, 0, 3, 0, 16)
+        load_scales(nc.sync, 0, 1, 0, 16)
+        load_scales(nc.sync, 0, 2, 0, 16)
+        nc.sync.dma_start(w8_raw[:], w8.rearrange("(p j) n -> p j n", j=PACK))
+        nc.sync.dma_start(words[1][:], table_words[1])
+        nc.sync.dma_start(w4_codes[:].bitcast(I32), w4_words[0].bitcast(I32))
+        for q in range(4):
+            load_w4_scales(nc.sync, q)
         nc.scalar.activation(warm[:], warm[:], COPY)
 
-        nc.vector.tensor_copy(picked[1][:], words[1][:].bitcast(U32).indirect(offsets[:]))
+        nc.vector.tensor_copy(picked[0][:], words[0][:].bitcast(U32).indirect(offsets[:]))
         nc.vector.tensor_copy(picked_planes[:], planes[:].indirect(offsets[:]))
         for m in range(2):
             cols = slice(m * P, (m + 1) * P)
             nc.scalar.copy(w8_grouped[:, cols, :], w8_raw[:, :, cols].rearrange("p j n -> p n j"))
-        for m in range(2):
-            cols = slice(m * P, (m + 1) * P)
             nc.vector.quantize_mx(
                 out=w8_codes[:, cols].bitcast(E4M3),
                 scales=w8_plane[:, cols],
                 in_=w8_grouped[:, cols, :].rearrange("p n j -> p (n j)"),
             )
-
-        for c in range(4):
-            for m in range(2):
+            for c in range(4):
                 nc.tensor.matmul_mx(
                     out=sums[m][c][:],
-                    lhsT=w4_codes[:, 2 * m * P : 2 * (m + 1) * P].bitcast(E2M1),
-                    lhsT_scale=w4_plane[:, m * P : (m + 1) * P],
-                    rhs=picked[1][:, c * P : (c + 1) * P].bitcast(E4M3),
-                    rhs_scale=picked_planes[:, c * P : (c + 1) * P],
+                    lhsT=w8_codes[:, cols].bitcast(E4M3),
+                    lhsT_scale=w8_plane[:, cols],
+                    rhs=picked[0][:, c * P : (c + 1) * P].bitcast(E4M3),
+                    rhs_scale=picked_planes[4:P, c * P : (c + 1) * P],
                     start=True,
                     stop=False,
                 )
         for c in range(4):
             cols = slice(c * P, (c + 1) * P)
-            nc.vector.tensor_copy(picked[0][:, cols], words[0][:].bitcast(U32).indirect(offsets[:, 8 * c : 8 * (c + 1)]))
+            nc.vector.tensor_copy(picked[1][:, cols], words[1][:].bitcast(U32).indirect(offsets[:, 8 * c : 8 * (c + 1)]))
             for m in range(2):
                 nc.tensor.matmul_mx(
                     out=sums[m][c][:],
-                    lhsT=w8_codes[:, m * P : (m + 1) * P].bitcast(E4M3),
-                    lhsT_scale=w8_plane[:, m * P : (m + 1) * P],
-                    rhs=picked[0][:, cols].bitcast(E4M3),
-                    rhs_scale=picked_planes[4:P, cols],
+                    lhsT=w4_codes[:, 2 * m * P : 2 * (m + 1) * P].bitcast(E2M1),
+                    lhsT_scale=w4_plane[:, m * P : (m + 1) * P],
+                    rhs=picked[1][:, cols].bitcast(E4M3),
+                    rhs_scale=picked_planes[:, cols],
                     start=False,
                     stop=True,
                 )

from contextlib import ExitStack

import concourse.mybir as mybir

F32 = mybir.dt.float32
BF16 = mybir.dt.bfloat16
U32 = mybir.dt.uint32
I32 = mybir.dt.int32
U16 = mybir.dt.uint16
U8 = mybir.dt.uint8
E4M3 = mybir.dt.float8_e4m3fn_x4
E2M1 = mybir.dt.float4_e2m1fn_x4
COPY = mybir.ActivationFunctionType.Copy

O, K, M, T, S = 512, 1024, 256, 1024, 512
P = 128
PACK = 4
FLOPS = 2 * K * M * S


def tile_list_tabo_none_kernel(tc, tab, w8, w4_words, w4_scales, offs, out):
    nc = tc.nc
    with ExitStack() as ctx:
        keep = ctx.enter_context(tc.tile_pool(name="keep", bufs=1))
        psum = ctx.enter_context(tc.psum_pool(name="psum", bufs=1))

        offsets = keep.tile([P, S // 16], U16, name="offsets")
        words = [keep.tile([P, T], I32, name=f"words{a}", align_bytes=64) for a in range(2)]
        planes = keep.tile([P, T], U8, name="planes", align_bytes=64)
        w8_raw = keep.tile([P, PACK, M], F32, name="w8_raw", align_bytes=64)
        w8_grouped = keep.tile([P, M, PACK], BF16, name="w8_grouped", align_bytes=64)
        w8_codes = keep.tile([P, M], U32, name="w8_codes", align_bytes=64)
        w8_plane = keep.tile([P, M], U8, name="w8_plane", align_bytes=64)
        w4_codes = keep.tile([P, 2 * M], U8, name="w4_codes", align_bytes=64)
        w4_plane = keep.tile([P, M], U8, name="w4_plane", align_bytes=64)
        picked = [keep.tile([P, S], U32, name=f"picked{a}", align_bytes=64) for a in range(2)]
        picked_planes = keep.tile([P, S], U8, name="picked_planes", align_bytes=64)
        warm = keep.tile([P, 1], F32, name="warm")
        results = [keep.tile([P, S], F32, name=f"result{m}", align_bytes=64) for m in range(2)]
        sums = [[psum.tile([P, P], F32, name=f"sum{m}_{c}") for c in range(4)] for m in range(2)]

        table_words = [tab[a, 0 : 4 * P * T].rearrange("(p b) -> p b", b=4 * T).bitcast(I32) for a in range(2)]
        table_scales = [tab[a, 4 * P * T : 4 * P * T + 16 * T].rearrange("(q t) -> q t", t=T).bitcast(I32) for a in range(2)]

        nc.vector.memset(warm[:], 0.0)

        flat = tab.rearrange("a b -> (a b)")

        def load_scales(queue, a, q, before, rows):
            first = 32 * q + 4 * (1 - a) - before
            start = a * (4 * P + 16) * T + 4 * P * T + (4 * q - before) * T
            queue.dma_start(
                planes[first : first + rows, :].bitcast(I32),
                flat[start : start + rows * T].rearrange("(r t) -> r t", t=T).bitcast(I32),
            )

        def load_w4_scales(queue, q):
            queue.dma_start(w4_plane[32 * q : 32 * q + 4, :].bitcast(I32), w4_scales[0, 4 * q : 4 * q + 4, :].bitcast(I32))

        nc.vector.memset(planes[96:P, :].bitcast(I32), 0)
        nc.sync.dma_start(offsets[:], offs)
        load_scales(nc.scalar, 1, 0, 0, 4)
        load_scales(nc.sync, 1, 1, 12, 16)
        load_scales(nc.scalar, 1, 2, 12, 16)
        load_scales(nc.sync, 0, 0, 0, 16)
        load_scales(nc.scalar, 1, 3, 12, 16)
        nc.sync.dma_start(words[0][:], table_words[0])
        load_scales(nc.scalar, 0, 3, 0, 16)
        load_scales(nc.sync, 0, 1, 0, 16)
        load_scales(nc.sync, 0, 2, 0, 16)
        nc.sync.dma_start(w8_raw[:], w8.rearrange("(p j) n -> p j n", j=PACK))
        nc.sync.dma_start(words[1][:], table_words[1])
        nc.sync.dma_start(w4_codes[:].bitcast(I32), w4_words[0].bitcast(I32))
        for q in range(4):
            load_w4_scales(nc.sync, q)
        nc.scalar.activation(warm[:], warm[:], COPY)

        nc.vector.tensor_copy(picked[0][:], words[0][:].bitcast(U32).indirect(offsets[:]))
        nc.vector.tensor_copy(picked_planes[:], planes[:].indirect(offsets[:]))
        for m in range(2):
            cols = slice(m * P, (m + 1) * P)
            nc.scalar.copy(w8_grouped[:, cols, :], w8_raw[:, :, cols].rearrange("p j n -> p n j"))
            nc.vector.quantize_mx(
                out=w8_codes[:, cols].bitcast(E4M3),
                scales=w8_plane[:, cols],
                in_=w8_grouped[:, cols, :].rearrange("p n j -> p (n j)"),
            )
            for c in range(4):
                nc.tensor.matmul_mx(
                    out=sums[m][c][:],
                    lhsT=w8_codes[:, cols].bitcast(E4M3),
                    lhsT_scale=w8_plane[:, cols],
                    rhs=picked[0][:, c * P : (c + 1) * P].bitcast(E4M3),
                    rhs_scale=picked_planes[4:P, c * P : (c + 1) * P],
                    start=True,
                    stop=False,
                )
        for c in range(4):
            cols = slice(c * P, (c + 1) * P)
            nc.vector.tensor_copy(picked[1][:, cols], words[1][:].bitcast(U32).indirect(offsets[:, 8 * c : 8 * (c + 1)]))
            for m in range(2):
                nc.tensor.matmul_mx(
                    out=sums[m][c][:],
                    lhsT=w4_codes[:, 2 * m * P : 2 * (m + 1) * P].bitcast(E2M1),
                    lhsT_scale=w4_plane[:, m * P : (m + 1) * P],
                    rhs=picked[1][:, cols].bitcast(E4M3),
                    rhs_scale=picked_planes[:, cols],
                    start=False,
                    stop=True,
                )
            nc.scalar.copy(results[0][:, cols], sums[0][c][:])
            if c < 3:
                nc.scalar.copy(results[1][:, cols], sums[1][c][:])
            else:
                nc.vector.tensor_copy(results[1][:, cols], sums[1][c][:])
            if c == 2:
                for m in range(2):
                    nc.sync.dma_start(out[m * P : (m + 1) * P, 0 : 3 * P], results[m][:, 0 : 3 * P])
        nc.scalar.dma_start(out[0:P, 3 * P : S], results[0][:, 3 * P : S])
        nc.sync.dma_start(out[P : 2 * P, 3 * P : S], results[1][:, 3 * P : S])
